import numpy as np
import ml_dtypes


def mxq(x, axis, fmt="e4m3"):
    dtype, down = {"e4m3": (ml_dtypes.float8_e4m3fn, 7), "e5m2": (ml_dtypes.float8_e5m2, 14)}[fmt]
    v = np.moveaxis(np.asarray(x, np.float32).astype(ml_dtypes.bfloat16).astype(np.float64), axis, -1)
    blocks = v.reshape(v.shape[:-1] + (-1, 32))
    amax = np.abs(blocks).max(-1, keepdims=True)
    byte = np.maximum(np.where(amax > 0, np.frexp(amax)[1] - 1 + 127, 0) - down, 1)
    scale = np.exp2(byte - 127.0)
    codes = (blocks / scale).astype(np.float32).astype(dtype).astype(np.float64)
    return np.moveaxis((codes * scale).reshape(v.shape), -1, axis)


WIDE = False


def mx_kscale(k):
    if not WIDE:
        return np.ones(k)
    levels = np.array([10, -10, 5, -5, 0])
    if k % 512:
        return np.exp2(np.random.permutation(np.resize(levels, k // 32))).repeat(32)
    a = np.empty((k // 512, 16))
    for p in range(k // 512):
        a[p, :8] = np.random.permutation(np.resize(levels, 8))
        for g in range(8):
            far = levels[np.abs(levels - a[p, g]) >= 10]
            a[p, g + 8] = far[np.random.randint(len(far))]
    return np.exp2(a.ravel()).repeat(32)


BF16 = ml_dtypes.bfloat16


def bf(x):
    return np.asarray(x, np.float32).astype(BF16)


def f64(x):
    return np.asarray(x).astype(np.float64)


E2M1 = np.array([0.0, 0.5, 1.0, 1.5, 2.0, 3.0, 4.0, 6.0, -0.0, -0.5, -1.0, -1.5, -2.0, -3.0, -4.0, -6.0])


def pack_weight(w, fmt):
    k, n = w.shape
    w = f64(bf(w)).reshape(k // 32, 32, n)
    amax = np.abs(w).max(1)
    if fmt == "e4m3":
        byte = np.frexp(amax)[1] - 1 + 127 - 7
    else:
        mant, ex = np.frexp(amax / 6.0)
        byte = np.where(mant > 0.5, ex, ex - 1) + 127
    byte = np.clip(np.where(amax > 0, byte, 1), 1, 254)
    scaled = (w * np.exp2(127.0 - byte)[:, None, :]).reshape(k, n).astype(np.float32)
    by_word = np.ascontiguousarray(scaled.reshape(k // 512, 128, 4, n).transpose(0, 1, 3, 2))
    if fmt == "e4m3":
        words = by_word.astype(ml_dtypes.float8_e4m3fn).view(np.uint8)
    else:
        c = by_word.astype(ml_dtypes.float4_e2m1fn).view(np.uint8) & 0xF
        words = c[..., 0::2] | (c[..., 1::2] << 4)
    return np.ascontiguousarray(words), np.ascontiguousarray(byte.astype(np.uint8).reshape(k // 512, 16, n))


def unpack_weight(words, scales, fmt):
    g, p, n, _ = words.shape
    if fmt == "e4m3":
        vals = np.ascontiguousarray(words).view(ml_dtypes.float8_e4m3fn).astype(np.float64)
    else:
        nib = np.empty((g, p, n, 4), np.uint8)
        nib[..., 0::2] = words & 0xF
        nib[..., 1::2] = words >> 4
        vals = E2M1[nib]
    vals = vals * np.repeat(np.exp2(scales.astype(np.float64) - 127.0), 8, axis=1)[..., None]
    return vals.transpose(0, 1, 3, 2).reshape(g * 512, n)
def pack4(w):
    words, scales = pack_weight(w, "e2m1")
    return words.reshape(words.shape[0], 128, -1), scales


def unpack4(words, scales):
    return unpack_weight(words.reshape(words.shape[0], 128, -1, 2), scales, "e2m1")


T, H, C, R, D = 2048, 512, 1536, 512, 2560


def draw0():
    s = mx_kscale(H)
    r = mx_kscale(C)
    t = mx_kscale(T)
    b_rest = np.random.standard_normal((C, R)) / np.sqrt(H + C) / r[:, None]
    b_rest_words, b_rest_scales = pack4(b_rest)
    x = np.random.standard_normal((T, D)) / np.sqrt(T) / t[:, None]
    x_words, x_scales = pack4(x)
    return {"dy_hot": bf(2 * np.random.standard_normal((T, H)) * s),
            "b_hot": bf(np.random.standard_normal((H, R)) / np.sqrt(H + C) / s[:, None]),
            "dy_rest": bf(np.random.standard_normal((T, C)) * r),
            "b_rest_words": b_rest_words,
            "b_rest_scales": b_rest_scales,
            "lam": bf(1 + 0.1 * np.random.standard_normal(R)),
            "token_w": bf(np.random.uniform(0.5, 1.5, T) * t),
            "x_words": x_words,
            "x_scales": x_scales}


def core(dy_hot, b_hot, dy_rest, b_rest_words, b_rest_scales, lam, token_w, x_words, x_scales):
    hot = mxq(f64(dy_hot), 1, "e4m3") @ mxq(f64(b_hot), 0, "e4m3")
    rest = mxq(f64(dy_rest), 1, "e4m3") @ unpack4(b_rest_words, b_rest_scales)
    g = (hot + rest) * f64(lam) * f64(token_w)[:, None]
    x = unpack4(x_words, x_scales)
    da = x.T @ mxq(g, 0, "e4m3")
    return da


def e4m3fn_bytes(y):
    return np.clip(np.asarray(y, np.float64), -448.0, 448.0).astype(np.float32).astype(ml_dtypes.float8_e4m3fn).view(np.uint8)


def e4m3fn_values(b):
    return np.asarray(b, np.uint8).view(ml_dtypes.float8_e4m3fn).astype(np.float64)


def setup_inputs():
    d = draw0()
    x0 = np.asarray(d['dy_rest']).astype(np.float64)
    s = (np.max(np.abs(x0), axis=(0,), keepdims=True) / 448.0).astype(np.float32)
    out = {}
    for k, v in d.items():
        if k == 'dy_rest':
            out['dy_rest_bytes'] = e4m3fn_bytes(x0 / s.astype(np.float64))
            out['dy_rest_scale'] = s
        else:
            out[k] = v
    return out


def reference(dy_hot, b_hot, dy_rest_bytes, dy_rest_scale, b_rest_words, b_rest_scales, lam, token_w, x_words, x_scales):
    return core(dy_hot, b_hot, e4m3fn_values(dy_rest_bytes) * dy_rest_scale.astype(np.float64), b_rest_words, b_rest_scales, lam, token_w, x_words, x_scales)

@@ -1,0 +1,308 @@
+from contextlib import ExitStack
+
+import concourse.mybir as mybir
+from concourse.masks import make_identity
+
+T, H, C, R, D = 2048, 512, 1536, 512, 2560
+FLOPS = 2 * T * (H + C) * R + 2 * D * T * R
+
+F32 = mybir.dt.float32
+BF16 = mybir.dt.bfloat16
+I32 = mybir.dt.int32
+U32 = mybir.dt.uint32
+U8 = mybir.dt.uint8
+FP8 = mybir.dt.float8_e4m3fn
+FP8X4 = mybir.dt.float8_e4m3fn_x4
+FP4X4 = mybir.dt.float4_e2m1fn_x4
+MULT = mybir.AluOpType.mult
+ADD = mybir.AluOpType.add
+COPY = mybir.ActivationFunctionType.Copy
+
+P = 128
+PACK = 4
+GROUPS = T // 512
+PHASES = 4
+STEPS = GROUPS * PHASES
+PASSES = (H + C) // 512
+RBLOCKS = R // 128
+DTILES = D // 128
+OPEN_TILES = 4
+PERM_REST = ()
+PERM_HOT = ()
+
+
+def tile_lora_down_gradient_s3_kernel(
+    tc, dy_hot, b_hot, dy_rest_bytes, dy_rest_scale, b_rest_words, b_rest_scales, lam, token_w, x_words, x_scales, out
+):
+    nc = tc.nc
+
+    with ExitStack() as ctx:
+        keep = ctx.enter_context(tc.tile_pool(name="keep", bufs=1))
+        work = ctx.enter_context(tc.tile_pool(name="work", bufs=3))
+        psum = ctx.enter_context(tc.psum_pool(name="psum", bufs=1))
+        ctx.enter_context(tc.manual_schedule())
+
+        ident = keep.tile([P, P], F32, name="ident")
+        scale_all = keep.tile([P, C], F32, name="scale_all", align_bytes=64)
+        w_bf = keep.tile([P, GROUPS, PHASES], BF16, name="w_bf", align_bytes=64)
+        w_col = keep.tile([P, GROUPS, PHASES], F32, name="w_col", align_bytes=64)
+        lam_all = keep.tile([P, R], BF16, name="lam_all", align_bytes=64)
+        b_raw = keep.tile([P, PACK, R], BF16, name="b_raw", align_bytes=64)
+        b_grouped = keep.tile([P, R, PACK], BF16, name="b_grouped", align_bytes=64)
+        bh_codes = keep.tile([P, R], U32, name="bh_codes", align_bytes=64)
+        bh_scales = keep.tile([P, R], U8, name="bh_scales", align_bytes=64)
+        bw = keep.tile([P, C // 512, 2 * R], U8, name="bw", align_bytes=64)
+        bs = keep.tile([P, C // 512, R], U8, name="bs", align_bytes=64)
+        xw = keep.tile([P, GROUPS, 2 * D], U8, name="xw", align_bytes=64)
+        xs = keep.tile([P, GROUPS, D], U8, name="xs", align_bytes=64)
+        factor = keep.tile([P, GROUPS, PHASES, R], F32, name="factor", align_bytes=64)
+        g_codes = keep.tile([P, GROUPS, R], U32, name="g_codes", align_bytes=64)
+        g_scales = keep.tile([P, GROUPS, R], U8, name="g_scales", align_bytes=64)
+        codes8 = [keep.tile([P, PHASES, C], U8, name="codes8_%d" % g, align_bytes=64) for g in range(GROUPS)]
+        hot = [keep.tile([P, PHASES, H], BF16, name="hot_%d" % g, align_bytes=64) for g in range(GROUPS)]
+        result = [keep.tile([P, R], F32, name="result_%d" % d, align_bytes=64) for d in range(DTILES)]
+
+        bytes_v = dy_rest_bytes.rearrange("(g m t) k -> g m t k", m=P, t=PHASES)
+        hot_v = dy_hot.rearrange("(g m t) k -> g m t k", m=P, t=PHASES)
+        scale_v = dy_rest_scale.rearrange("o k -> (o k)")
+
+        nc.vector.memset(bs[:].rearrange("p g n -> p (g n)").bitcast(I32), 0)
+        nc.vector.memset(xs[:].rearrange("p g n -> p (g n)").bitcast(I32), 0)
+        make_identity(nc, ident[:])
+
+        def load_scale(c):
+            cols = slice(512 * c, 512 * (c + 1))
+            nc.sync.dma_start(out=scale_all[:, cols], in_=scale_v[cols].partition_broadcast(P))
+
+        def load_bytes(g, t0, t1):
+            nc.sync.dma_start(out=codes8[g][:, t0:t1, :], in_=bytes_v[g][:, t0:t1, :])
+
+        def load_hot(g, t0, t1):
+            nc.sync.dma_start(out=hot[g][:, t0:t1, :], in_=hot_v[g][:, t0:t1, :])
+
+        def load_scale_rows(dst, src):
+            for q in range(4):
+                nc.sync.dma_start(
+                    out=dst[32 * q : 32 * q + 4, :, :].bitcast(I32),
+                    in_=src[:, 4 * q : 4 * q + 4, :].rearrange("g q n -> q g n").bitcast(I32),
+                )
+
+        load_scale(0)
+        load_bytes(0, 0, 1)
+        nc.scalar.dma_start(out=w_bf[:], in_=token_w.rearrange("(g m t) -> m g t", m=P, t=PHASES))
+        nc.scalar.dma_start(out=lam_all[:], in_=lam.partition_broadcast(P))
+        load_scale(1)
+        load_scale(2)
+        load_hot(0, 0, 1)
+        load_bytes(0, 1, 2)
+        load_hot(0, 1, 2)
+        load_bytes(0, 2, 4)
+        nc.sync.dma_start(out=b_raw[:], in_=b_hot.rearrange("(p j) n -> p j n", j=PACK))
+        load_hot(0, 2, 4)
+        nc.sync.dma_start(out=bw[:].bitcast(I32), in_=b_rest_words.rearrange("g p b -> p g b").bitcast(I32))
+        load_scale_rows(bs, b_rest_scales)
+        for g in range(1, GROUPS):
+            load_bytes(g, 0, 2)
+            load_hot(g, 0, 4)
+            load_bytes(g, 2, 4)
+        load_scale_rows(xs, x_scales)
+        for g in range(GROUPS):
+            nc.sync.dma_start(out=xw[:, g, :].bitcast(I32), in_=x_words[g].bitcast(I32))
+
+        widened = {}
+        grouped = {}
+        dy_codes = {}
+        dy_scales = {}
+        acc = {}
+
+        def product(s):
+            g, t = divmod(s, PHASES)
+            widened[s] = work.tile([P, C], BF16, name="widened", align_bytes=64)
+            cuts = (0, 512, 1024, C) if s == 0 else (0, 512, C)
+            for k0, k1 in zip(cuts[:-1], cuts[1:]):
+                nc.vector.tensor_tensor(
+                    out=widened[s][:, k0:k1],
+                    in0=codes8[g][:, t, k0:k1].bitcast(FP8),
+                    in1=scale_all[:, k0:k1],
+                    op=MULT,
+                )
+
+        sorted_rest = {}
+        sorted_hot = {}
+
+        def sort_words(s):
+            g, t = divmod(s, PHASES)
+            if s in PERM_REST:
+                sorted_rest[s] = work.tile([P, 3, 2, P], F32, name="sorted_rest", align_bytes=64, bufs=2)
+                nc.scalar.copy(out=sorted_rest[s][:], in_=widened[s][:].bitcast(F32).rearrange("p (c q u) -> p c u q", c=3, u=2))
+            if s in PERM_HOT:
+                sorted_hot[s] = work.tile([P, 2, P], F32, name="sorted_hot", align_bytes=64, bufs=2)
+                nc.scalar.copy(out=sorted_hot[s][:], in_=hot[g][:, t, :].bitcast(F32).rearrange("p (q u) -> p u q", u=2))
+
+        def turn(s):
+            g, t = divmod(s, PHASES)
+            rest_words = widened[s][:].bitcast(F32)
+            hot_words = hot[g][:, t, :].bitcast(F32)
+            pr = sorted_rest.get(s)
+            ph = sorted_hot.get(s)
+            grouped[s] = work.tile([P, PASSES, P, PACK], BF16, name="grouped", align_bytes=64)
+            words_out = grouped[s][:].bitcast(F32)
+            for h in range(2):
+                bank = psum.tile([P, 2, 2, P], F32, name="turned", tag="turned", bufs=2)
+                for i in range(2):
+                    c = 2 * h + i
+                    words, base = (hot_words, 0) if c == 0 else (rest_words, 256 * (c - 1))
+                    for u in range(2):
+                        if c == 0 and ph is not None:
+                            src = ph[:, u, :]
+                        elif c > 0 and pr is not None:
+                            src = pr[:, c - 1, u, :]
+                        else:
+                            src = words[:, base + u : base + 256 : 2]
+                        nc.tensor.transpose(bank[:, i, u, :], src, ident[:])
+                nc.scalar.copy(out=words_out[:, 2 * h : 2 * h + 2, :, :], in_=bank[:].rearrange("p c u n -> p c n u"))
+
+        def quantise(s):
+            dy_codes[s] = work.tile([P, PASSES, P], U32, name="dy_codes", align_bytes=64)
+            dy_scales[s] = work.tile([P, PASSES, P], U8, name="dy_scales", align_bytes=64)
+            nc.vector.quantize_mx(
+                out=dy_codes[s][:].rearrange("p c n -> p (c n)").bitcast(FP8X4),
+                scales=dy_scales[s][:].rearrange("p c n -> p (c n)"),
+                in_=grouped[s][:].rearrange("p c n t -> p (c n t)"),
+            )
+
+        def stage1(s):
+            t = s % PHASES
+            for j in range(RBLOCKS):
+                if t == 0:
+                    acc[j] = psum.tile([P, PHASES, 128], F32, name="acc_%d" % j, tag="acc_%d" % j, bufs=1)
+                for c in range(PASSES):
+                    if c == 0:
+                        rhs = bh_codes[:, 128 * j : 128 * (j + 1)].bitcast(FP8X4)
+                        rhs_scale = bh_scales[:, 128 * j : 128 * (j + 1)]
+                    else:
+                        rhs = bw[:, c - 1, 256 * j : 256 * (j + 1)].bitcast(FP4X4)
+                        rhs_scale = bs[:, c - 1, 128 * j : 128 * (j + 1)]
+                    nc.tensor.matmul_mx(
+                        out=acc[j][:, t, :],
+                        lhsT=dy_codes[s][:, c, :].bitcast(FP8X4),
+                        lhsT_scale=dy_scales[s][:, c, :],
+                        rhs=rhs,
+                        rhs_scale=rhs_scale,
+                        start=(c == 0),
+                        stop=(c == PASSES - 1),
+                    )
+
+        def make_factor(n):
+            g, t = divmod(n, PHASES)
+            nc.scalar.activation(out=factor[:, g, t, :], in_=lam_all[:], func=COPY, scale=w_col[:, g, t : t + 1])
+
+        weighted_of = {}
+
+        def weigh(g):
+            weighted = weighted_of[g] = work.tile([P, R, PHASES], BF16, name="weighted", align_bytes=64, bufs=2)
+            for j in range(RBLOCKS):
+                nc.vector.tensor_tensor(
+                    out=weighted[:, 128 * j : 128 * (j + 1), :],
+                    in0=acc[j][:].rearrange("p t r -> p r t"),
+                    in1=factor[:, g, :, 128 * j : 128 * (j + 1)].rearrange("p t r -> p r t"),
+                    op=MULT,
+                )
+
+        def quantise_g(g):
+            weighted = weighted_of[g]
+            parts = 4 if g == GROUPS - 1 else 1
+            w = R // parts
+            for n in range(parts):
+                cols = slice(w * n, w * (n + 1))
+                nc.vector.quantize_mx(
+                    out=g_codes[:, g, cols].bitcast(FP8X4),
+                    scales=g_scales[:, g, cols],
+                    in_=weighted[:, cols, :].rearrange("p r t -> p (r t)"),
+                )
+
+        def stage2(bank, d, groups, first, last):
+            for g in groups:
+                nc.tensor.matmul_mx(
+                    out=bank[:],
+                    lhsT=xw[:, g, 256 * d : 256 * (d + 1)].bitcast(FP4X4),
+                    lhsT_scale=xs[:, g, 128 * d : 128 * (d + 1)],
+                    rhs=g_codes[:, g, :].bitcast(FP8X4),
+                    rhs_scale=g_scales[:, g, :],
+                    start=(g == first),
+                    stop=(g == last),
+                )
+
+        def early_half(d):
+            bank = psum.tile([P, R], F32, name="out_bank", tag="out_bank", bufs=2)
+            stage2(bank, d, (0, 1), 0, 1)
+            nc.scalar.copy(out=result[d][:], in_=bank[:])
+
+        def store(d):
+            nc.sync.dma_start(out=out[128 * d : 128 * (d + 1), :], in_=result[d][:])
+
+        nc.scalar.copy(out=w_col[:], in_=w_bf[:])
+        early = list(range(OPEN_TILES, DTILES))
+        early_count = {12: 3, 13: 2, 14: 2, 15: 2, 16: 3, 17: 2, 18: 2}
+        factors = {0: 1, 1: 1, 2: 1, 3: 1, 4: 1, 5: 1, 6: 1, 7: 1, 8: 1, 9: 1, 10: 1, 11: 1, 12: 1, 13: 1, 14: 1, 15: 1}
+        nf = 0
+        open_banks = []
+        tags = ["turned", "turned", "out_bank", "out_bank"]
+
+        def b_part(h):
+            cols = slice(256 * h, 256 * (h + 1))
+            nc.scalar.copy(out=b_grouped[:, cols, :], in_=b_raw[:, :, cols].rearrange("p j n -> p n j"))
+
+        for n in range(STEPS + 3):
+            ne = early_count.get(n, 0)
+            if n < STEPS:
+                product(n)
+            if 1 <= n <= STEPS:
+                turn(n - 1)
+            if n < STEPS:
+                sort_words(n)
+            if n in (1, 2):
+                b_part(n - 1)
+            if n == 3:
+                nc.vector.quantize_mx(
+                    out=bh_codes[:].bitcast(FP8X4),
+                    scales=bh_scales[:],
+                    in_=b_grouped[:].rearrange("p n j -> p (n j)"),
+                )
+            if n % PHASES == 3 and n >= 7:
+                weigh((n - 7) // PHASES)
+                quantise_g((n - 7) // PHASES)
+            if 2 <= n < STEPS + 2:
+                quantise(n - 2)
+
+            if ne > 2:
+                early_half(early[0])
+                early = early[1:]
+            if 3 <= n < STEPS + 3:
+                stage1(n - 3)
+            for i in range(factors.get(n, 0)):
+                make_factor(nf)
+                nf += 1
+            for i in range(ne - (1 if ne > 2 else 0)):
+                early_half(early[0])
+                early = early[1:]
+        weigh(3)
+        quantise_g(3)
+
+
+        for d in range(OPEN_TILES):
+            bank = psum.tile([P, R], F32, name="open_bank", tag=tags[d], bufs=2)
+            stage2(bank, d, (0, 1, 2), 0, 3)
+            open_banks.append(bank)
+        rest = list(range(OPEN_TILES, DTILES))
+        for i in range(len(rest)):
+            d = rest[i]
+            if i < OPEN_TILES:
+                stage2(open_banks[i], i, (3,), 0, 3)
+                nc.scalar.copy(out=result[i][:], in_=open_banks[i][:])
+                store(i)
+            tag = "acc_%d" % (i % 4)
+            bank = psum.tile([P, R], F32, name="late_bank", tag=tag, bufs=1)
+            stage2(bank, d, (2, 3), 2, 3)
+            nc.vector.tensor_tensor(out=result[d][:], in0=bank[:], in1=result[d][:], op=ADD)
+            store(d)

@@ -46,7 +46,10 @@ def tile_lora_down_gradient_s3_kernel(
         scale_all = keep.tile([P, C], F32, name="scale_all", align_bytes=64)
         w_bf = keep.tile([P, GROUPS, PHASES], BF16, name="w_bf", align_bytes=64)
         w_col = keep.tile([P, GROUPS, PHASES], F32, name="w_col", align_bytes=64)
-        lam_all = keep.tile([P, R], BF16, name="lam_all", align_bytes=64)
+        lam_bf = keep.tile([P, PACK], BF16, name="lam_bf", align_bytes=64)
+        lam_col = keep.tile([P, PACK], F32, name="lam_col", align_bytes=64)
+        lam_all = keep.tile([P, R], F32, name="lam_all", align_bytes=64)
+        scale_col = keep.tile([P, C // 512, PACK], F32, name="scale_col", align_bytes=64)
         b_raw = keep.tile([P, PACK, R], BF16, name="b_raw", align_bytes=64)
         b_grouped = keep.tile([P, R, PACK], BF16, name="b_grouped", align_bytes=64)
         bh_codes = keep.tile([P, R], U32, name="bh_codes", align_bytes=64)
@@ -70,10 +73,6 @@ def tile_lora_down_gradient_s3_kernel(
         nc.vector.memset(xs[:].rearrange("p g n -> p (g n)").bitcast(I32), 0)
         make_identity(nc, ident[:])
 
-        def load_scale(c):
-            cols = slice(512 * c, 512 * (c + 1))
-            nc.sync.dma_start(out=scale_all[:, cols], in_=scale_v[cols].partition_broadcast(P))
-
         def load_bytes(g, t0, t1):
             nc.sync.dma_start(out=codes8[g][:, t0:t1, :], in_=bytes_v[g][:, t0:t1, :])
 
@@ -87,12 +86,10 @@ def tile_lora_down_gradient_s3_kernel(
                     in_=src[:, 4 * q : 4 * q + 4, :].rearrange("g q n -> q g n").bitcast(I32),
                 )
 
-        load_scale(0)
+        nc.scalar.dma_start(out=scale_col[:], in_=scale_v.rearrange("(c p m) -> p c m", p=P, m=PACK))
         load_bytes(0, 0, 1)
+        nc.scalar.dma_start(out=lam_bf[:], in_=lam.rearrange("(p m) -> p m", m=PACK))
         nc.scalar.dma_start(out=w_bf[:], in_=token_w.rearrange("(g m t) -> m g t", m=P, t=PHASES))
-        nc.scalar.dma_start(out=lam_all[:], in_=lam.partition_broadcast(P))
-        load_scale(1)
-        load_scale(2)
         load_hot(0, 0, 1)
         load_bytes(0, 1, 2)
         load_hot(0, 1, 2)
@@ -233,18 +230,28 @@ def tile_lora_down_gradient_s3_kernel(
                     stop=(g == last),
                 )
 
+        def prefix(d):
+            return 1 if d < OPEN_TILES + 12 else 2
+
         def early_half(d):
             bank = psum.tile([P, R], F32, name="out_bank", tag="out_bank", bufs=2)
-            stage2(bank, d, (0, 1), 0, 1)
+            stage2(bank, d, range(prefix(d)), 0, prefix(d) - 1)
             nc.scalar.copy(out=result[d][:], in_=bank[:])
 
         def store(d):
             nc.sync.dma_start(out=out[128 * d : 128 * (d + 1), :], in_=result[d][:])
 
-        nc.scalar.copy(out=w_col[:], in_=w_bf[:])
+        def spread(dst, column, tag):
+            bank = psum.tile([P, PACK, P], F32, name="spread_bank", tag=tag, bufs=1)
+            for m in range(PACK):
+                nc.tensor.transpose(bank[:, m, :], column[:, m : m + 1].to_broadcast([P, P]), ident[:])
+            nc.scalar.copy(out=dst.rearrange("p (n m) -> p n m", m=PACK), in_=bank[:].rearrange("p m n -> p n m"))
+
+        for c in range(C // 512):
+            spread(scale_all[:, 512 * c : 512 * (c + 1)], scale_col[:, c, :], "acc_%d" % c)
         early = list(range(OPEN_TILES, DTILES))
-        early_count = {12: 3, 13: 2, 14: 2, 15: 2, 16: 3, 17: 2, 18: 2}
-        factors = {0: 1, 1: 1, 2: 1, 3: 1, 4: 1, 5: 1, 6: 1, 7: 1, 8: 1, 9: 1, 10: 1, 11: 1, 12: 1, 13: 1, 14: 1, 15: 1}
+        early_count = {8: 1, 9: 2, 10: 1, 11: 2, 12: 2, 13: 1, 14: 2, 15: 1, 16: 2, 17: 2}
+        factors = {1: 1, 2: 2, 3: 1, 4: 1, 5: 1, 6: 1, 7: 1, 8: 1, 9: 1, 10: 1, 11: 1, 12: 1, 13: 1, 14: 1, 15: 1}
         nf = 0
         open_banks = []
         tags = ["turned", "turned", "out_bank", "out_bank"]
@@ -259,21 +266,25 @@ def tile_lora_down_gradient_s3_kernel(
                 product(n)
             if 1 <= n <= STEPS:
                 turn(n - 1)
+            if n == 1:
+                nc.scalar.copy(out=lam_col[:], in_=lam_bf[:])
+                nc.scalar.copy(out=w_col[:], in_=w_bf[:])
+                spread(lam_all[:], lam_col[:], "acc_3")
             if n < STEPS:
                 sort_words(n)
             if n in (1, 2):
                 b_part(n - 1)
+            if n % PHASES == 3 and n >= 7:
+                weigh((n - 7) // PHASES)
+                quantise_g((n - 7) // PHASES)
+            if 2 <= n < STEPS + 2:
+                quantise(n - 2)
             if n == 3:
                 nc.vector.quantize_mx(
                     out=bh_codes[:].bitcast(FP8X4),
                     scales=bh_scales[:],
                     in_=b_grouped[:].rearrange("p n j -> p (n j)"),
                 )
-            if n % PHASES == 3 and n >= 7:
-                weigh((n - 7) // PHASES)
-                quantise_g((n - 7) // PHASES)
-            if 2 <= n < STEPS + 2:
-                quantise(n - 2)
 
             if ne > 2:
                 early_half(early[0])
@@ -303,6 +314,6 @@ def tile_lora_down_gradient_s3_kernel(
                 store(i)
             tag = "acc_%d" % (i % 4)
             bank = psum.tile([P, R], F32, name="late_bank", tag=tag, bufs=1)
-            stage2(bank, d, (2, 3), 2, 3)
+            stage2(bank, d, range(prefix(d), GROUPS), prefix(d), GROUPS - 1)
             nc.vector.tensor_tensor(out=result[d][:], in0=bank[:], in1=result[d][:], op=ADD)
             store(d)

@@ -20,15 +20,14 @@ COPY = mybir.ActivationFunctionType.Copy
 
 P = 128
 PACK = 4
-GROUPS = T // 512
-PHASES = 4
-STEPS = GROUPS * PHASES
-PASSES = (H + C) // 512
-RBLOCKS = R // 128
-DTILES = D // 128
-OPEN_TILES = 4
-PERM_REST = ()
-PERM_HOT = ()
+K_PASS = P * PACK
+GROUPS = T // K_PASS
+PHASES = PACK
+TILES = GROUPS * PHASES
+REST = C // K_PASS
+OUT_TILES = D // P
+OPEN = 4
+SHORT = 12
 
 
 def tile_lora_down_gradient_s3_kernel(
@@ -39,129 +38,134 @@ def tile_lora_down_gradient_s3_kernel(
     with ExitStack() as ctx:
         keep = ctx.enter_context(tc.tile_pool(name="keep", bufs=1))
         work = ctx.enter_context(tc.tile_pool(name="work", bufs=3))
-        psum = ctx.enter_context(tc.psum_pool(name="psum", bufs=1))
+        psum = ctx.enter_context(tc.psum_pool(name="psum", bufs=2))
         ctx.enter_context(tc.manual_schedule())
 
         ident = keep.tile([P, P], F32, name="ident")
-        scale_all = keep.tile([P, C], F32, name="scale_all", align_bytes=64)
-        w_bf = keep.tile([P, GROUPS, PHASES], BF16, name="w_bf", align_bytes=64)
-        w_col = keep.tile([P, GROUPS, PHASES], F32, name="w_col", align_bytes=64)
+        weight_bf = keep.tile([P, GROUPS, PHASES], BF16, name="weight_bf", align_bytes=64)
+        weight = keep.tile([P, GROUPS, PHASES], F32, name="weight", align_bytes=64)
         lam_bf = keep.tile([P, PACK], BF16, name="lam_bf", align_bytes=64)
         lam_col = keep.tile([P, PACK], F32, name="lam_col", align_bytes=64)
         lam_all = keep.tile([P, R], F32, name="lam_all", align_bytes=64)
-        scale_col = keep.tile([P, C // 512, PACK], F32, name="scale_col", align_bytes=64)
+        scale = keep.tile([P, REST, PACK], F32, name="scale", align_bytes=64)
         b_raw = keep.tile([P, PACK, R], BF16, name="b_raw", align_bytes=64)
         b_grouped = keep.tile([P, R, PACK], BF16, name="b_grouped", align_bytes=64)
-        bh_codes = keep.tile([P, R], U32, name="bh_codes", align_bytes=64)
-        bh_scales = keep.tile([P, R], U8, name="bh_scales", align_bytes=64)
-        bw = keep.tile([P, C // 512, 2 * R], U8, name="bw", align_bytes=64)
-        bs = keep.tile([P, C // 512, R], U8, name="bs", align_bytes=64)
-        xw = keep.tile([P, GROUPS, 2 * D], U8, name="xw", align_bytes=64)
-        xs = keep.tile([P, GROUPS, D], U8, name="xs", align_bytes=64)
-        factor = keep.tile([P, GROUPS, PHASES, R], F32, name="factor", align_bytes=64)
+        b_hot_codes = keep.tile([P, R], U32, name="b_hot_codes", align_bytes=64)
+        b_hot_scales = keep.tile([P, R], U8, name="b_hot_scales", align_bytes=64)
+        b_words = keep.tile([P, REST, 2 * R], U8, name="b_words", align_bytes=64)
+        b_scales = keep.tile([P, REST, R], U8, name="b_scales", align_bytes=64)
+        xt_words = keep.tile([P, GROUPS, 2 * D], U8, name="xt_words", align_bytes=64)
+        xt_scales = keep.tile([P, GROUPS, D], U8, name="xt_scales", align_bytes=64)
         g_codes = keep.tile([P, GROUPS, R], U32, name="g_codes", align_bytes=64)
         g_scales = keep.tile([P, GROUPS, R], U8, name="g_scales", align_bytes=64)
-        codes8 = [keep.tile([P, PHASES, C], U8, name="codes8_%d" % g, align_bytes=64) for g in range(GROUPS)]
+        rest_bytes = [keep.tile([P, PHASES, C], U8, name="rest_bytes_%d" % g, align_bytes=64) for g in range(GROUPS)]
         hot = [keep.tile([P, PHASES, H], BF16, name="hot_%d" % g, align_bytes=64) for g in range(GROUPS)]
-        result = [keep.tile([P, R], F32, name="result_%d" % d, align_bytes=64) for d in range(DTILES)]
+        result = [keep.tile([P, R], F32, name="result_%d" % d, align_bytes=64) for d in range(OUT_TILES)]
 
-        bytes_v = dy_rest_bytes.rearrange("(g m t) k -> g m t k", m=P, t=PHASES)
-        hot_v = dy_hot.rearrange("(g m t) k -> g m t k", m=P, t=PHASES)
-        scale_v = dy_rest_scale.rearrange("o k -> (o k)")
-
-        nc.vector.memset(bs[:].rearrange("p g n -> p (g n)").bitcast(I32), 0)
-        nc.vector.memset(xs[:].rearrange("p g n -> p (g n)").bitcast(I32), 0)
+        nc.vector.memset(b_scales[:].rearrange("p g n -> p (g n)").bitcast(I32), 0)
+        nc.vector.memset(xt_scales[:].rearrange("p g n -> p (g n)").bitcast(I32), 0)
         make_identity(nc, ident[:])
 
+        bytes_hbm = dy_rest_bytes.rearrange("(g m t) k -> g m t k", m=P, t=PHASES)
+        hot_hbm = dy_hot.rearrange("(g m t) k -> g m t k", m=P, t=PHASES)
+
         def load_bytes(g, t0, t1):
-            nc.sync.dma_start(out=codes8[g][:, t0:t1, :], in_=bytes_v[g][:, t0:t1, :])
+            nc.sync.dma_start(out=rest_bytes[g][:, t0:t1, :], in_=bytes_hbm[g][:, t0:t1, :])
 
         def load_hot(g, t0, t1):
-            nc.sync.dma_start(out=hot[g][:, t0:t1, :], in_=hot_v[g][:, t0:t1, :])
+            nc.sync.dma_start(out=hot[g][:, t0:t1, :], in_=hot_hbm[g][:, t0:t1, :])
 
-        def load_scale_rows(dst, src):
+        def load_scale_rows(tile, hbm):
             for q in range(4):
                 nc.sync.dma_start(
-                    out=dst[32 * q : 32 * q + 4, :, :].bitcast(I32),
-                    in_=src[:, 4 * q : 4 * q + 4, :].rearrange("g q n -> q g n").bitcast(I32),
+                    out=tile[32 * q : 32 * q + 4, :, :].bitcast(I32),
+                    in_=hbm[:, 4 * q : 4 * q + 4, :].rearrange("g q n -> q g n").bitcast(I32),
                 )
 
-        nc.scalar.dma_start(out=scale_col[:], in_=scale_v.rearrange("(c p m) -> p c m", p=P, m=PACK))
         load_bytes(0, 0, 1)
-        nc.scalar.dma_start(out=lam_bf[:], in_=lam.rearrange("(p m) -> p m", m=PACK))
-        nc.scalar.dma_start(out=w_bf[:], in_=token_w.rearrange("(g m t) -> m g t", m=P, t=PHASES))
-        load_hot(0, 0, 1)
+        nc.scalar.dma_start(out=scale[:], in_=dy_rest_scale.rearrange("o (c p t) -> p (o c) t", p=P, t=PACK))
+        load_hot(0, 0, 2)
         load_bytes(0, 1, 2)
-        load_hot(0, 1, 2)
+        nc.scalar.dma_start(out=lam_bf[:], in_=lam.rearrange("(p i) -> p i", i=PACK))
         load_bytes(0, 2, 4)
-        nc.sync.dma_start(out=b_raw[:], in_=b_hot.rearrange("(p j) n -> p j n", j=PACK))
+        nc.scalar.dma_start(out=weight_bf[:], in_=token_w.rearrange("(g m t) -> m g t", m=P, t=PHASES))
+        nc.sync.dma_start(out=b_raw[:], in_=b_hot.rearrange("(p t) n -> p t n", t=PACK))
         load_hot(0, 2, 4)
-        nc.sync.dma_start(out=bw[:].bitcast(I32), in_=b_rest_words.rearrange("g p b -> p g b").bitcast(I32))
-        load_scale_rows(bs, b_rest_scales)
+        nc.sync.dma_start(out=b_words[:].bitcast(I32), in_=b_rest_words.rearrange("g p b -> p g b").bitcast(I32))
+        load_scale_rows(b_scales, b_rest_scales)
         for g in range(1, GROUPS):
             load_bytes(g, 0, 2)
             load_hot(g, 0, 4)
             load_bytes(g, 2, 4)
-        load_scale_rows(xs, x_scales)
+        load_scale_rows(xt_scales, x_scales)
         for g in range(GROUPS):
-            nc.sync.dma_start(out=xw[:, g, :].bitcast(I32), in_=x_words[g].bitcast(I32))
+            nc.sync.dma_start(out=xt_words[:, g, :].bitcast(I32), in_=x_words[g].bitcast(I32))
+
+        def spread_lam():
+            nc.scalar.copy(out=lam_col[:], in_=lam_bf[:])
+            nc.scalar.copy(out=weight[:], in_=weight_bf[:])
+            bank = psum.tile([P, PACK, P], F32, name="lam_bank", tag="out_bank")
+            for i in range(PACK):
+                nc.tensor.transpose(bank[:, i, :], lam_col[:, i : i + 1].to_broadcast([P, P]), ident[:])
+            nc.scalar.copy(out=lam_all[:].rearrange("p (n i) -> p n i", i=PACK), in_=bank[:].rearrange("p i n -> p n i"))
+
+        def interleave_b_hot():
+            nc.gpsimd.tensor_scalar(
+                out=b_grouped[:],
+                in0=b_raw[:].rearrange("p t n -> p n t"),
+                scalar1=1.0,
+                scalar2=0.0,
+                op0=MULT,
+                op1=ADD,
+            )
+
+        def quantise_b_hot():
+            nc.vector.quantize_mx(
+                out=b_hot_codes[:].bitcast(FP8X4),
+                scales=b_hot_scales[:],
+                in_=b_grouped[:].rearrange("p n t -> p (n t)"),
+            )
 
         widened = {}
+        banks = {}
         grouped = {}
         dy_codes = {}
         dy_scales = {}
-        acc = {}
+        sums = {}
+        weighted = {}
 
-        def product(s):
+        def widen(s):
             g, t = divmod(s, PHASES)
-            widened[s] = work.tile([P, C], BF16, name="widened", align_bytes=64)
-            cuts = (0, 512, 1024, C) if s == 0 else (0, 512, C)
-            for k0, k1 in zip(cuts[:-1], cuts[1:]):
-                nc.vector.tensor_tensor(
-                    out=widened[s][:, k0:k1],
-                    in0=codes8[g][:, t, k0:k1].bitcast(FP8),
-                    in1=scale_all[:, k0:k1],
-                    op=MULT,
-                )
-
-        sorted_rest = {}
-        sorted_hot = {}
-
-        def sort_words(s):
-            g, t = divmod(s, PHASES)
-            if s in PERM_REST:
-                sorted_rest[s] = work.tile([P, 3, 2, P], F32, name="sorted_rest", align_bytes=64, bufs=2)
-                nc.scalar.copy(out=sorted_rest[s][:], in_=widened[s][:].bitcast(F32).rearrange("p (c q u) -> p c u q", c=3, u=2))
-            if s in PERM_HOT:
-                sorted_hot[s] = work.tile([P, 2, P], F32, name="sorted_hot", align_bytes=64, bufs=2)
-                nc.scalar.copy(out=sorted_hot[s][:], in_=hot[g][:, t, :].bitcast(F32).rearrange("p (q u) -> p u q", u=2))
+            widened[s] = work.tile([P, C], BF16, name="widened", align_bytes=64, bufs=4)
+            nc.scalar.copy(out=widened[s][:], in_=rest_bytes[g][:, t, :].bitcast(FP8))
 
         def turn(s):
             g, t = divmod(s, PHASES)
             rest_words = widened[s][:].bitcast(F32)
             hot_words = hot[g][:, t, :].bitcast(F32)
-            pr = sorted_rest.get(s)
-            ph = sorted_hot.get(s)
-            grouped[s] = work.tile([P, PASSES, P, PACK], BF16, name="grouped", align_bytes=64)
-            words_out = grouped[s][:].bitcast(F32)
-            for h in range(2):
-                bank = psum.tile([P, 2, 2, P], F32, name="turned", tag="turned", bufs=2)
-                for i in range(2):
-                    c = 2 * h + i
-                    words, base = (hot_words, 0) if c == 0 else (rest_words, 256 * (c - 1))
-                    for u in range(2):
-                        if c == 0 and ph is not None:
-                            src = ph[:, u, :]
-                        elif c > 0 and pr is not None:
-                            src = pr[:, c - 1, u, :]
-                        else:
-                            src = words[:, base + u : base + 256 : 2]
-                        nc.tensor.transpose(bank[:, i, u, :], src, ident[:])
-                nc.scalar.copy(out=words_out[:, 2 * h : 2 * h + 2, :, :], in_=bank[:].rearrange("p c u n -> p c n u"))
+            banks[s] = [psum.tile([P, 2, 2, P], F32, name="turned", tag="turned", bufs=4) for h in range(2)]
+            for c in range(REST + 1):
+                words = hot_words if c == REST else rest_words[:, 256 * c : 256 * (c + 1)]
+                for u in range(2):
+                    nc.tensor.transpose(banks[s][c // 2][:, c % 2, u, :], words[:, u:256:2], ident[:])
+            grouped[s] = work.tile([P, REST + 1, P, PACK], BF16, name="grouped", align_bytes=64, bufs=5)
+            nc.scalar.copy(
+                out=grouped[s][:, REST, :, :].bitcast(F32),
+                in_=banks[s][1][:, 1, :, :].rearrange("p u n -> p n u"),
+            )
 
-        def quantise(s):
-            dy_codes[s] = work.tile([P, PASSES, P], U32, name="dy_codes", align_bytes=64)
-            dy_scales[s] = work.tile([P, PASSES, P], U8, name="dy_scales", align_bytes=64)
+        def product(s):
+            for c in range(REST):
+                nc.vector.tensor_tensor(
+                    out=grouped[s][:, c, :, :].rearrange("p n (u e) -> p n u e", u=2),
+                    in0=banks[s][c // 2][:, c % 2, :, :].bitcast(BF16).rearrange("p u (n e) -> p n u e", e=2),
+                    in1=scale[:, c, :].unsqueeze(1).to_broadcast([P, P, PACK]).rearrange("p n (u e) -> p n u e", u=2),
+                    op=MULT,
+                )
+
+        def quantise_dy(s):
+            dy_codes[s] = work.tile([P, REST + 1, P], U32, name="dy_codes", align_bytes=64)
+            dy_scales[s] = work.tile([P, REST + 1, P], U8, name="dy_scales", align_bytes=64)
             nc.vector.quantize_mx(
                 out=dy_codes[s][:].rearrange("p c n -> p (c n)").bitcast(FP8X4),
                 scales=dy_scales[s][:].rearrange("p c n -> p (c n)"),
@@ -169,151 +173,111 @@ def tile_lora_down_gradient_s3_kernel(
             )
 
         def stage1(s):
-            t = s % PHASES
-            for j in range(RBLOCKS):
-                if t == 0:
-                    acc[j] = psum.tile([P, PHASES, 128], F32, name="acc_%d" % j, tag="acc_%d" % j, bufs=1)
-                for c in range(PASSES):
-                    if c == 0:
-                        rhs = bh_codes[:, 128 * j : 128 * (j + 1)].bitcast(FP8X4)
-                        rhs_scale = bh_scales[:, 128 * j : 128 * (j + 1)]
-                    else:
-                        rhs = bw[:, c - 1, 256 * j : 256 * (j + 1)].bitcast(FP4X4)
-                        rhs_scale = bs[:, c - 1, 128 * j : 128 * (j + 1)]
-                    nc.tensor.matmul_mx(
-                        out=acc[j][:, t, :],
-                        lhsT=dy_codes[s][:, c, :].bitcast(FP8X4),
-                        lhsT_scale=dy_scales[s][:, c, :],
-                        rhs=rhs,
-                        rhs_scale=rhs_scale,
-                        start=(c == 0),
-                        stop=(c == PASSES - 1),
-                    )
+            g, t = divmod(s, PHASES)
+            bank = psum.tile([P, R], F32, name="acc", tag="acc")
+            for c in range(REST + 1):
+                is_hot = c == REST
+                nc.tensor.matmul_mx(
+                    out=bank[:],
+                    lhsT=dy_codes[s][:, c, :].bitcast(FP8X4),
+                    lhsT_scale=dy_scales[s][:, c, :],
+                    rhs=b_hot_codes[:].bitcast(FP8X4) if is_hot else b_words[:, c, :].bitcast(FP4X4),
+                    rhs_scale=b_hot_scales[:] if is_hot else b_scales[:, c, :],
+                    start=(c == 0),
+                    stop=is_hot,
+                )
+            if t == 0:
+                sums[g] = work.tile([P, PHASES, R], F32, name="sums", align_bytes=64, bufs=2)
+            nc.scalar.activation(out=sums[g][:, t, :], in_=bank[:], func=COPY, scale=weight[:, g, t : t + 1])
 
-        def make_factor(n):
-            g, t = divmod(n, PHASES)
-            nc.scalar.activation(out=factor[:, g, t, :], in_=lam_all[:], func=COPY, scale=w_col[:, g, t : t + 1])
-
-        weighted_of = {}
-
-        def weigh(g):
-            weighted = weighted_of[g] = work.tile([P, R, PHASES], BF16, name="weighted", align_bytes=64, bufs=2)
-            for j in range(RBLOCKS):
-                nc.vector.tensor_tensor(
-                    out=weighted[:, 128 * j : 128 * (j + 1), :],
-                    in0=acc[j][:].rearrange("p t r -> p r t"),
-                    in1=factor[:, g, :, 128 * j : 128 * (j + 1)].rearrange("p t r -> p r t"),
+        def weigh(g, engine):
+            weighted[g] = work.tile([P, R, PHASES], BF16, name="weighted", align_bytes=64, bufs=2)
+            for r0 in range(0, R, P):
+                cols = slice(r0, r0 + P)
+                engine.tensor_tensor(
+                    out=weighted[g][:, cols, :],
+                    in0=sums[g][:, :, cols].rearrange("p t r -> p r t"),
+                    in1=lam_all[:, cols].unsqueeze(2).to_broadcast([P, P, PHASES]),
                     op=MULT,
                 )
 
-        def quantise_g(g):
-            weighted = weighted_of[g]
-            parts = 4 if g == GROUPS - 1 else 1
-            w = R // parts
-            for n in range(parts):
-                cols = slice(w * n, w * (n + 1))
+        def quantise_g(g, width):
+            for r0 in range(0, R, width):
+                cols = slice(r0, r0 + width)
                 nc.vector.quantize_mx(
                     out=g_codes[:, g, cols].bitcast(FP8X4),
                     scales=g_scales[:, g, cols],
-                    in_=weighted[:, cols, :].rearrange("p r t -> p (r t)"),
+                    in_=weighted[g][:, cols, :].rearrange("p r t -> p (r t)"),
                 )
 
         def stage2(bank, d, groups, first, last):
             for g in groups:
                 nc.tensor.matmul_mx(
                     out=bank[:],
-                    lhsT=xw[:, g, 256 * d : 256 * (d + 1)].bitcast(FP4X4),
-                    lhsT_scale=xs[:, g, 128 * d : 128 * (d + 1)],
+                    lhsT=xt_words[:, g, 2 * P * d : 2 * P * (d + 1)].bitcast(FP4X4),
+                    lhsT_scale=xt_scales[:, g, P * d : P * (d + 1)],
                     rhs=g_codes[:, g, :].bitcast(FP8X4),
                     rhs_scale=g_scales[:, g, :],
                     start=(g == first),
                     stop=(g == last),
                 )
 
-        def prefix(d):
-            return 1 if d < OPEN_TILES + 12 else 2
+        def early_groups(d):
+            return 1 if d < OPEN + SHORT else 2
 
-        def early_half(d):
-            bank = psum.tile([P, R], F32, name="out_bank", tag="out_bank", bufs=2)
-            stage2(bank, d, range(prefix(d)), 0, prefix(d) - 1)
+        def early_part(d):
+            bank = psum.tile([P, R], F32, name="early", tag="out_bank")
+            stage2(bank, d, range(early_groups(d)), 0, early_groups(d) - 1)
             nc.scalar.copy(out=result[d][:], in_=bank[:])
 
         def store(d):
-            nc.sync.dma_start(out=out[128 * d : 128 * (d + 1), :], in_=result[d][:])
+            nc.sync.dma_start(out=out[P * d : P * (d + 1), :], in_=result[d][:])
 
-        def spread(dst, column, tag):
-            bank = psum.tile([P, PACK, P], F32, name="spread_bank", tag=tag, bufs=1)
-            for m in range(PACK):
-                nc.tensor.transpose(bank[:, m, :], column[:, m : m + 1].to_broadcast([P, P]), ident[:])
-            nc.scalar.copy(out=dst.rearrange("p (n m) -> p n m", m=PACK), in_=bank[:].rearrange("p m n -> p n m"))
-
-        for c in range(C // 512):
-            spread(scale_all[:, 512 * c : 512 * (c + 1)], scale_col[:, c, :], "acc_%d" % c)
-        early = list(range(OPEN_TILES, DTILES))
-        early_count = {8: 1, 9: 2, 10: 1, 11: 2, 12: 2, 13: 1, 14: 2, 15: 1, 16: 2, 17: 2}
-        factors = {1: 1, 2: 2, 3: 1, 4: 1, 5: 1, 6: 1, 7: 1, 8: 1, 9: 1, 10: 1, 11: 1, 12: 1, 13: 1, 14: 1, 15: 1}
-        nf = 0
-        open_banks = []
-        tags = ["turned", "turned", "out_bank", "out_bank"]
-
-        def b_part(h):
-            cols = slice(256 * h, 256 * (h + 1))
-            nc.scalar.copy(out=b_grouped[:, cols, :], in_=b_raw[:, :, cols].rearrange("p j n -> p n j"))
-
-        for n in range(STEPS + 3):
-            ne = early_count.get(n, 0)
-            if n < STEPS:
+        widen(0)
+        widen(1)
+        first_early, last_step = 8, TILES + 1
+        done = OPEN
+        for n in range(TILES + 2):
+            if n % 2 == 0 and n < TILES:
+                for s in (n, n + 1):
+                    turn(s)
+                    if s + 2 < TILES:
+                        widen(s + 2)
+            if n == 0:
+                spread_lam()
+            if n < TILES:
                 product(n)
-            if 1 <= n <= STEPS:
-                turn(n - 1)
-            if n == 1:
-                nc.scalar.copy(out=lam_col[:], in_=lam_bf[:])
-                nc.scalar.copy(out=w_col[:], in_=w_bf[:])
-                spread(lam_all[:], lam_col[:], "acc_3")
-            if n < STEPS:
-                sort_words(n)
-            if n in (1, 2):
-                b_part(n - 1)
-            if n % PHASES == 3 and n >= 7:
-                weigh((n - 7) // PHASES)
-                quantise_g((n - 7) // PHASES)
-            if 2 <= n < STEPS + 2:
-                quantise(n - 2)
-            if n == 3:
-                nc.vector.quantize_mx(
-                    out=bh_codes[:].bitcast(FP8X4),
-                    scales=bh_scales[:],
-                    in_=b_grouped[:].rearrange("p n j -> p (n j)"),
-                )
+            if n == 0:
+                interleave_b_hot()
+            if 1 <= n <= TILES:
+                quantise_dy(n - 1)
+            if n == 2:
+                quantise_b_hot()
+            if n >= 2:
+                stage1(n - 2)
+            if n % PHASES == 1 and 5 <= n < TILES:
+                weigh(n // PHASES - 1, nc.gpsimd)
+            if n % PHASES == 0 and 8 <= n <= TILES:
+                quantise_g(n // PHASES - 2, R)
+            while done - OPEN < (n + 1 - first_early) * (OUT_TILES - OPEN) // (last_step + 1 - first_early):
+                early_part(done)
+                done += 1
 
-            if ne > 2:
-                early_half(early[0])
-                early = early[1:]
-            if 3 <= n < STEPS + 3:
-                stage1(n - 3)
-            for i in range(factors.get(n, 0)):
-                make_factor(nf)
-                nf += 1
-            for i in range(ne - (1 if ne > 2 else 0)):
-                early_half(early[0])
-                early = early[1:]
-        weigh(3)
-        quantise_g(3)
+        weigh(GROUPS - 1, nc.vector)
+        quantise_g(GROUPS - 1, P)
 
-
-        for d in range(OPEN_TILES):
-            bank = psum.tile([P, R], F32, name="open_bank", tag=tags[d], bufs=2)
-            stage2(bank, d, (0, 1, 2), 0, 3)
-            open_banks.append(bank)
-        rest = list(range(OPEN_TILES, DTILES))
-        for i in range(len(rest)):
-            d = rest[i]
-            if i < OPEN_TILES:
-                stage2(open_banks[i], i, (3,), 0, 3)
-                nc.scalar.copy(out=result[i][:], in_=open_banks[i][:])
+        waiting = []
+        for d in range(OPEN):
+            bank = psum.tile([P, R], F32, name="waiting_bank", tag="turned", bufs=4)
+            stage2(bank, d, range(GROUPS - 1), 0, GROUPS - 1)
+            waiting.append(bank)
+        for i in range(OUT_TILES - OPEN):
+            if i < OPEN:
+                stage2(waiting[i], i, (GROUPS - 1,), 0, GROUPS - 1)
+                nc.scalar.copy(out=result[i][:], in_=waiting[i][:])
                 store(i)
-            tag = "acc_%d" % (i % 4)
-            bank = psum.tile([P, R], F32, name="late_bank", tag=tag, bufs=1)
-            stage2(bank, d, range(prefix(d), GROUPS), prefix(d), GROUPS - 1)
+            d = OPEN + i
+            bank = psum.tile([P, R], F32, name="late", tag=("acc", "out_bank")[i % 2])
+            stage2(bank, d, range(early_groups(d), GROUPS), early_groups(d), GROUPS - 1)
             nc.vector.tensor_tensor(out=result[d][:], in0=bank[:], in1=result[d][:], op=ADD)
             store(d)

@@ -28,6 +28,7 @@ REST = C // K_PASS
 OUT_TILES = D // P
 OPEN = 4
 SHORT = 12
+GPSIMD_WIDTH = 64
 
 
 def tile_lora_down_gradient_s3_kernel(
@@ -42,28 +43,28 @@ def tile_lora_down_gradient_s3_kernel(
         ctx.enter_context(tc.manual_schedule())
 
         ident = keep.tile([P, P], F32, name="ident")
-        weight_bf = keep.tile([P, GROUPS, PHASES], BF16, name="weight_bf", align_bytes=64)
-        weight = keep.tile([P, GROUPS, PHASES], F32, name="weight", align_bytes=64)
+        token_weight_bf = keep.tile([P, GROUPS, PHASES], BF16, name="token_weight_bf", align_bytes=64)
+        token_weight = keep.tile([P, GROUPS, PHASES], F32, name="token_weight", align_bytes=64)
         lam_bf = keep.tile([P, PACK], BF16, name="lam_bf", align_bytes=64)
         lam_col = keep.tile([P, PACK], F32, name="lam_col", align_bytes=64)
         lam_all = keep.tile([P, R], F32, name="lam_all", align_bytes=64)
-        scale = keep.tile([P, REST, PACK], F32, name="scale", align_bytes=64)
+        channel_scale = keep.tile([P, REST, PACK], F32, name="channel_scale", align_bytes=64)
         b_raw = keep.tile([P, PACK, R], BF16, name="b_raw", align_bytes=64)
         b_grouped = keep.tile([P, R, PACK], BF16, name="b_grouped", align_bytes=64)
         b_hot_codes = keep.tile([P, R], U32, name="b_hot_codes", align_bytes=64)
         b_hot_scales = keep.tile([P, R], U8, name="b_hot_scales", align_bytes=64)
-        b_words = keep.tile([P, REST, 2 * R], U8, name="b_words", align_bytes=64)
-        b_scales = keep.tile([P, REST, R], U8, name="b_scales", align_bytes=64)
-        xt_words = keep.tile([P, GROUPS, 2 * D], U8, name="xt_words", align_bytes=64)
-        xt_scales = keep.tile([P, GROUPS, D], U8, name="xt_scales", align_bytes=64)
+        b_words_sb = keep.tile([P, REST, 2 * R], U8, name="b_words_sb", align_bytes=64)
+        b_scales_sb = keep.tile([P, REST, R], U8, name="b_scales_sb", align_bytes=64)
+        x_words_sb = keep.tile([P, GROUPS, 2 * D], U8, name="x_words_sb", align_bytes=64)
+        x_scales_sb = keep.tile([P, GROUPS, D], U8, name="x_scales_sb", align_bytes=64)
         g_codes = keep.tile([P, GROUPS, R], U32, name="g_codes", align_bytes=64)
         g_scales = keep.tile([P, GROUPS, R], U8, name="g_scales", align_bytes=64)
         rest_bytes = [keep.tile([P, PHASES, C], U8, name="rest_bytes_%d" % g, align_bytes=64) for g in range(GROUPS)]
         hot = [keep.tile([P, PHASES, H], BF16, name="hot_%d" % g, align_bytes=64) for g in range(GROUPS)]
         result = [keep.tile([P, R], F32, name="result_%d" % d, align_bytes=64) for d in range(OUT_TILES)]
 
-        nc.vector.memset(b_scales[:].rearrange("p g n -> p (g n)").bitcast(I32), 0)
-        nc.vector.memset(xt_scales[:].rearrange("p g n -> p (g n)").bitcast(I32), 0)
+        nc.vector.memset(b_scales_sb[:].rearrange("p g n -> p (g n)").bitcast(I32), 0)
+        nc.vector.memset(x_scales_sb[:].rearrange("p g n -> p (g n)").bitcast(I32), 0)
         make_identity(nc, ident[:])
 
         bytes_hbm = dy_rest_bytes.rearrange("(g m t) k -> g m t k", m=P, t=PHASES)
@@ -83,27 +84,27 @@ def tile_lora_down_gradient_s3_kernel(
                 )
 
         load_bytes(0, 0, 1)
-        nc.scalar.dma_start(out=scale[:], in_=dy_rest_scale.rearrange("o (c p t) -> p (o c) t", p=P, t=PACK))
+        nc.scalar.dma_start(out=channel_scale[:], in_=dy_rest_scale.rearrange("o (c p t) -> p (o c) t", p=P, t=PACK))
         load_hot(0, 0, 2)
         load_bytes(0, 1, 2)
         nc.scalar.dma_start(out=lam_bf[:], in_=lam.rearrange("(p i) -> p i", i=PACK))
         load_bytes(0, 2, 4)
-        nc.scalar.dma_start(out=weight_bf[:], in_=token_w.rearrange("(g m t) -> m g t", m=P, t=PHASES))
+        nc.scalar.dma_start(out=token_weight_bf[:], in_=token_w.rearrange("(g m t) -> m g t", m=P, t=PHASES))
         nc.sync.dma_start(out=b_raw[:], in_=b_hot.rearrange("(p t) n -> p t n", t=PACK))
         load_hot(0, 2, 4)
-        nc.sync.dma_start(out=b_words[:].bitcast(I32), in_=b_rest_words.rearrange("g p b -> p g b").bitcast(I32))
-        load_scale_rows(b_scales, b_rest_scales)
+        nc.sync.dma_start(out=b_words_sb[:].bitcast(I32), in_=b_rest_words.rearrange("g p b -> p g b").bitcast(I32))
+        load_scale_rows(b_scales_sb, b_rest_scales)
         for g in range(1, GROUPS):
             load_bytes(g, 0, 2)
             load_hot(g, 0, 4)
             load_bytes(g, 2, 4)
-        load_scale_rows(xt_scales, x_scales)
+        load_scale_rows(x_scales_sb, x_scales)
         for g in range(GROUPS):
-            nc.sync.dma_start(out=xt_words[:, g, :].bitcast(I32), in_=x_words[g].bitcast(I32))
+            nc.sync.dma_start(out=x_words_sb[:, g, :].bitcast(I32), in_=x_words[g].bitcast(I32))
 
         def spread_lam():
             nc.scalar.copy(out=lam_col[:], in_=lam_bf[:])
-            nc.scalar.copy(out=weight[:], in_=weight_bf[:])
+            nc.scalar.copy(out=token_weight[:], in_=token_weight_bf[:])
             bank = psum.tile([P, PACK, P], F32, name="lam_bank", tag="out_bank")
             for i in range(PACK):
                 nc.tensor.transpose(bank[:, i, :], lam_col[:, i : i + 1].to_broadcast([P, P]), ident[:])
@@ -130,7 +131,7 @@ def tile_lora_down_gradient_s3_kernel(
         banks = {}
         grouped = {}
         dy_codes = {}
-        dy_scales = {}
+        dy_code_scales = {}
         sums = {}
         weighted = {}
 
@@ -159,16 +160,16 @@ def tile_lora_down_gradient_s3_kernel(
                 nc.vector.tensor_tensor(
                     out=grouped[s][:, c, :, :].rearrange("p n (u e) -> p n u e", u=2),
                     in0=banks[s][c // 2][:, c % 2, :, :].bitcast(BF16).rearrange("p u (n e) -> p n u e", e=2),
-                    in1=scale[:, c, :].unsqueeze(1).to_broadcast([P, P, PACK]).rearrange("p n (u e) -> p n u e", u=2),
+                    in1=channel_scale[:, c, :].unsqueeze(1).to_broadcast([P, P, PACK]).rearrange("p n (u e) -> p n u e", u=2),
                     op=MULT,
                 )
 
         def quantise_dy(s):
             dy_codes[s] = work.tile([P, REST + 1, P], U32, name="dy_codes", align_bytes=64)
-            dy_scales[s] = work.tile([P, REST + 1, P], U8, name="dy_scales", align_bytes=64)
+            dy_code_scales[s] = work.tile([P, REST + 1, P], U8, name="dy_code_scales", align_bytes=64)
             nc.vector.quantize_mx(
                 out=dy_codes[s][:].rearrange("p c n -> p (c n)").bitcast(FP8X4),
-                scales=dy_scales[s][:].rearrange("p c n -> p (c n)"),
+                scales=dy_code_scales[s][:].rearrange("p c n -> p (c n)"),
                 in_=grouped[s][:].rearrange("p c n t -> p (c n t)"),
             )
 
@@ -180,24 +181,24 @@ def tile_lora_down_gradient_s3_kernel(
                 nc.tensor.matmul_mx(
                     out=bank[:],
                     lhsT=dy_codes[s][:, c, :].bitcast(FP8X4),
-                    lhsT_scale=dy_scales[s][:, c, :],
-                    rhs=b_hot_codes[:].bitcast(FP8X4) if is_hot else b_words[:, c, :].bitcast(FP4X4),
-                    rhs_scale=b_hot_scales[:] if is_hot else b_scales[:, c, :],
+                    lhsT_scale=dy_code_scales[s][:, c, :],
+                    rhs=b_hot_codes[:].bitcast(FP8X4) if is_hot else b_words_sb[:, c, :].bitcast(FP4X4),
+                    rhs_scale=b_hot_scales[:] if is_hot else b_scales_sb[:, c, :],
                     start=(c == 0),
                     stop=is_hot,
                 )
             if t == 0:
                 sums[g] = work.tile([P, PHASES, R], F32, name="sums", align_bytes=64, bufs=2)
-            nc.scalar.activation(out=sums[g][:, t, :], in_=bank[:], func=COPY, scale=weight[:, g, t : t + 1])
+            nc.scalar.activation(out=sums[g][:, t, :], in_=bank[:], func=COPY, scale=token_weight[:, g, t : t + 1])
 
-        def weigh(g, engine):
+        def weigh(g, engine, width):
             weighted[g] = work.tile([P, R, PHASES], BF16, name="weighted", align_bytes=64, bufs=2)
-            for r0 in range(0, R, P):
-                cols = slice(r0, r0 + P)
+            for r0 in range(0, R, width):
+                cols = slice(r0, r0 + width)
                 engine.tensor_tensor(
                     out=weighted[g][:, cols, :],
                     in0=sums[g][:, :, cols].rearrange("p t r -> p r t"),
-                    in1=lam_all[:, cols].unsqueeze(2).to_broadcast([P, P, PHASES]),
+                    in1=lam_all[:, cols].unsqueeze(2).to_broadcast([P, width, PHASES]),
                     op=MULT,
                 )
 
@@ -214,8 +215,8 @@ def tile_lora_down_gradient_s3_kernel(
             for g in groups:
                 nc.tensor.matmul_mx(
                     out=bank[:],
-                    lhsT=xt_words[:, g, 2 * P * d : 2 * P * (d + 1)].bitcast(FP4X4),
-                    lhsT_scale=xt_scales[:, g, P * d : P * (d + 1)],
+                    lhsT=x_words_sb[:, g, 2 * P * d : 2 * P * (d + 1)].bitcast(FP4X4),
+                    lhsT_scale=x_scales_sb[:, g, P * d : P * (d + 1)],
                     rhs=g_codes[:, g, :].bitcast(FP8X4),
                     rhs_scale=g_scales[:, g, :],
                     start=(g == first),
@@ -256,14 +257,14 @@ def tile_lora_down_gradient_s3_kernel(
             if n >= 2:
                 stage1(n - 2)
             if n % PHASES == 1 and 5 <= n < TILES:
-                weigh(n // PHASES - 1, nc.gpsimd)
+                weigh(n // PHASES - 1, nc.gpsimd, GPSIMD_WIDTH)
             if n % PHASES == 0 and 8 <= n <= TILES:
                 quantise_g(n // PHASES - 2, R)
             while done - OPEN < (n + 1 - first_early) * (OUT_TILES - OPEN) // (last_step + 1 - first_early):
                 early_part(done)
                 done += 1
 
-        weigh(GROUPS - 1, nc.vector)
+        weigh(GROUPS - 1, nc.vector, P)
         quantise_g(GROUPS - 1, P)
 
         waiting = []

from contextlib import ExitStack

import concourse.mybir as mybir
from concourse.masks import make_identity

T, H, C, R, D = 2048, 512, 1536, 512, 2560
FLOPS = 2 * T * (H + C) * R + 2 * D * T * R

F32 = mybir.dt.float32
BF16 = mybir.dt.bfloat16
I32 = mybir.dt.int32
U32 = mybir.dt.uint32
U8 = mybir.dt.uint8
FP8 = mybir.dt.float8_e4m3fn
FP8X4 = mybir.dt.float8_e4m3fn_x4
FP4X4 = mybir.dt.float4_e2m1fn_x4
MULT = mybir.AluOpType.mult
ADD = mybir.AluOpType.add
COPY = mybir.ActivationFunctionType.Copy

P = 128
PACK = 4
K_PASS = P * PACK
GROUPS = T // K_PASS
PHASES = PACK
TILES = GROUPS * PHASES
REST = C // K_PASS
OUT_TILES = D // P
OPEN = 4
SHORT = 12
GPSIMD_WIDTH = 64


def tile_lora_down_gradient_s3_kernel(
    tc, dy_hot, b_hot, dy_rest_bytes, dy_rest_scale, b_rest_words, b_rest_scales, lam, token_w, x_words, x_scales, out
):
    nc = tc.nc

    with ExitStack() as ctx:
        keep = ctx.enter_context(tc.tile_pool(name="keep", bufs=1))
        work = ctx.enter_context(tc.tile_pool(name="work", bufs=3))
        psum = ctx.enter_context(tc.psum_pool(name="psum", bufs=2))
        ctx.enter_context(tc.manual_schedule())

        ident = keep.tile([P, P], F32, name="ident")
        token_weight_bf = keep.tile([P, GROUPS, PHASES], BF16, name="token_weight_bf", align_bytes=64)
        token_weight = keep.tile([P, GROUPS, PHASES], F32, name="token_weight", align_bytes=64)
        lam_bf = keep.tile([P, PACK], BF16, name="lam_bf", align_bytes=64)
        lam_col = keep.tile([P, PACK], F32, name="lam_col", align_bytes=64)
        lam_all = keep.tile([P, R], F32, name="lam_all", align_bytes=64)
        channel_scale = keep.tile([P, REST, PACK], F32, name="channel_scale", align_bytes=64)
        b_raw = keep.tile([P, PACK, R], BF16, name="b_raw", align_bytes=64)
        b_grouped = keep.tile([P, R, PACK], BF16, name="b_grouped", align_bytes=64)
        b_hot_codes = keep.tile([P, R], U32, name="b_hot_codes", align_bytes=64)
        b_hot_scales = keep.tile([P, R], U8, name="b_hot_scales", align_bytes=64)
        b_words_sb = keep.tile([P, REST, 2 * R], U8, name="b_words_sb", align_bytes=64)
        b_scales_sb = keep.tile([P, REST, R], U8, name="b_scales_sb", align_bytes=64)
        x_words_sb = keep.tile([P, GROUPS, 2 * D], U8, name="x_words_sb", align_bytes=64)
        x_scales_sb = keep.tile([P, GROUPS, D], U8, name="x_scales_sb", align_bytes=64)
        g_codes = keep.tile([P, GROUPS, R], U32, name="g_codes", align_bytes=64)
        g_scales = keep.tile([P, GROUPS, R], U8, name="g_scales", align_bytes=64)
        rest_bytes = [keep.tile([P, PHASES, C], U8, name="rest_bytes_%d" % g, align_bytes=64) for g in range(GROUPS)]
        hot = [keep.tile([P, PHASES, H], BF16, name="hot_%d" % g, align_bytes=64) for g in range(GROUPS)]
        result = [keep.tile([P, R], F32, name="result_%d" % d, align_bytes=64) for d in range(OUT_TILES)]

        nc.vector.memset(b_scales_sb[:].rearrange("p g n -> p (g n)").bitcast(I32), 0)
        nc.vector.memset(x_scales_sb[:].rearrange("p g n -> p (g n)").bitcast(I32), 0)
        make_identity(nc, ident[:])

        bytes_hbm = dy_rest_bytes.rearrange("(g m t) k -> g m t k", m=P, t=PHASES)
        hot_hbm = dy_hot.rearrange("(g m t) k -> g m t k", m=P, t=PHASES)

        def load_bytes(g, t0, t1):
            nc.sync.dma_start(out=rest_bytes[g][:, t0:t1, :], in_=bytes_hbm[g][:, t0:t1, :])

        def load_hot(g, t0, t1):
            nc.sync.dma_start(out=hot[g][:, t0:t1, :], in_=hot_hbm[g][:, t0:t1, :])

        def load_scale_rows(tile, hbm):
            for q in range(4):
                nc.sync.dma_start(
                    out=tile[32 * q : 32 * q + 4, :, :].bitcast(I32),
                    in_=hbm[:, 4 * q : 4 * q + 4, :].rearrange("g q n -> q g n").bitcast(I32),
                )

        load_bytes(0, 0, 1)
        nc.scalar.dma_start(out=channel_scale[:], in_=dy_rest_scale.rearrange("o (c p t) -> p (o c) t", p=P, t=PACK))
        load_hot(0, 0, 2)
        load_bytes(0, 1, 2)
        nc.scalar.dma_start(out=lam_bf[:], in_=lam.rearrange("(p i) -> p i", i=PACK))
        load_bytes(0, 2, 4)
        nc.scalar.dma_start(out=token_weight_bf[:], in_=token_w.rearrange("(g m t) -> m g t", m=P, t=PHASES))
        nc.sync.dma_start(out=b_raw[:], in_=b_hot.rearrange("(p t) n -> p t n", t=PACK))
        load_hot(0, 2, 4)
        nc.sync.dma_start(out=b_words_sb[:].bitcast(I32), in_=b_rest_words.rearrange("g p b -> p g b").bitcast(I32))
        load_scale_rows(b_scales_sb, b_rest_scales)
        for g in range(1, GROUPS):
            load_bytes(g, 0, 2)
            load_hot(g, 0, 4)
            load_bytes(g, 2, 4)
        load_scale_rows(x_scales_sb, x_scales)
        for g in range(GROUPS):
            nc.sync.dma_start(out=x_words_sb[:, g, :].bitcast(I32), in_=x_words[g].bitcast(I32))

        def spread_lam():
            nc.scalar.copy(out=lam_col[:], in_=lam_bf[:])
            nc.scalar.copy(out=token_weight[:], in_=token_weight_bf[:])
            bank = psum.tile([P, PACK, P], F32, name="lam_bank", tag="out_bank")
            for i in range(PACK):
                nc.tensor.transpose(bank[:, i, :], lam_col[:, i : i + 1].to_broadcast([P, P]), ident[:])
            nc.scalar.copy(out=lam_all[:].rearrange("p (n i) -> p n i", i=PACK), in_=bank[:].rearrange("p i n -> p n i"))

        def interleave_b_hot():
            nc.gpsimd.tensor_scalar(
                out=b_grouped[:],
                in0=b_raw[:].rearrange("p t n -> p n t"),
                scalar1=1.0,
                scalar2=0.0,
                op0=MULT,
                op1=ADD,
            )

        def quantise_b_hot():
            nc.vector.quantize_mx(
                out=b_hot_codes[:].bitcast(FP8X4),
                scales=b_hot_scales[:],
                in_=b_grouped[:].rearrange("p n t -> p (n t)"),
            )

        widened = {}
        banks = {}
        grouped = {}
        dy_codes = {}
        dy_code_scales = {}
        sums = {}
        weighted = {}

        def widen(s):
            g, t = divmod(s, PHASES)
            widened[s] = work.tile([P, C], BF16, name="widened", align_bytes=64, bufs=4)
            nc.scalar.copy(out=widened[s][:], in_=rest_bytes[g][:, t, :].bitcast(FP8))

        def turn(s):
            g, t = divmod(s, PHASES)
            rest_words = widened[s][:].bitcast(F32)
            hot_words = hot[g][:, t, :].bitcast(F32)
            banks[s] = [psum.tile([P, 2, 2, P], F32, name="turned", tag="turned", bufs=4) for h in range(2)]
            for c in range(REST + 1):
                words = hot_words if c == REST else rest_words[:, 256 * c : 256 * (c + 1)]
                for u in range(2):
                    nc.tensor.transpose(banks[s][c // 2][:, c % 2, u, :], words[:, u:256:2], ident[:])
            grouped[s] = work.tile([P, REST + 1, P, PACK], BF16, name="grouped", align_bytes=64, bufs=5)
            nc.scalar.copy(
                out=grouped[s][:, REST, :, :].bitcast(F32),
                in_=banks[s][1][:, 1, :, :].rearrange("p u n -> p n u"),
            )

        def product(s):
            for c in range(REST):
                nc.vector.tensor_tensor(
                    out=grouped[s][:, c, :, :].rearrange("p n (u e) -> p n u e", u=2),
                    in0=banks[s][c // 2][:, c % 2, :, :].bitcast(BF16).rearrange("p u (n e) -> p n u e", e=2),
                    in1=channel_scale[:, c, :].unsqueeze(1).to_broadcast([P, P, PACK]).rearrange("p n (u e) -> p n u e", u=2),
                    op=MULT,
                )

        def quantise_dy(s):
            dy_codes[s] = work.tile([P, REST + 1, P], U32, name="dy_codes", align_bytes=64)
            dy_code_scales[s] = work.tile([P, REST + 1, P], U8, name="dy_code_scales", align_bytes=64)
            nc.vector.quantize_mx(
                out=dy_codes[s][:].rearrange("p c n -> p (c n)").bitcast(FP8X4),
                scales=dy_code_scales[s][:].rearrange("p c n -> p (c n)"),
                in_=grouped[s][:].rearrange("p c n t -> p (c n t)"),
            )

        def stage1(s):
            g, t = divmod(s, PHASES)
            bank = psum.tile([P, R], F32, name="acc", tag="acc")
            for c in range(REST + 1):
                is_hot = c == REST
                nc.tensor.matmul_mx(
                    out=bank[:],
                    lhsT=dy_codes[s][:, c, :].bitcast(FP8X4),
                    lhsT_scale=dy_code_scales[s][:, c, :],
                    rhs=b_hot_codes[:].bitcast(FP8X4) if is_hot else b_words_sb[:, c, :].bitcast(FP4X4),
                    rhs_scale=b_hot_scales[:] if is_hot else b_scales_sb[:, c, :],
                    start=(c == 0),
                    stop=is_hot,
                )
            if t == 0:
                sums[g] = work.tile([P, PHASES, R], F32, name="sums", align_bytes=64, bufs=2)
            nc.scalar.activation(out=sums[g][:, t, :], in_=bank[:], func=COPY, scale=token_weight[:, g, t : t + 1])

        def weigh(g, engine, width):
            weighted[g] = work.tile([P, R, PHASES], BF16, name="weighted", align_bytes=64, bufs=2)
            for r0 in range(0, R, width):
                cols = slice(r0, r0 + width)
                engine.tensor_tensor(
                    out=weighted[g][:, cols, :],
                    in0=sums[g][:, :, cols].rearrange("p t r -> p r t"),
                    in1=lam_all[:, cols].unsqueeze(2).to_broadcast([P, width, PHASES]),
                    op=MULT,
                )

        def quantise_g(g, width):
            for r0 in range(0, R, width):
                cols = slice(r0, r0 + width)
                nc.vector.quantize_mx(
                    out=g_codes[:, g, cols].bitcast(FP8X4),
                    scales=g_scales[:, g, cols],
                    in_=weighted[g][:, cols, :].rearrange("p r t -> p (r t)"),
                )

        def stage2(bank, d, groups, first, last):
            for g in groups:
                nc.tensor.matmul_mx(
                    out=bank[:],
                    lhsT=x_words_sb[:, g, 2 * P * d : 2 * P * (d + 1)].bitcast(FP4X4),
                    lhsT_scale=x_scales_sb[:, g, P * d : P * (d + 1)],
                    rhs=g_codes[:, g, :].bitcast(FP8X4),
                    rhs_scale=g_scales[:, g, :],
                    start=(g == first),
                    stop=(g == last),
                )

        def early_groups(d):
            return 1 if d < OPEN + SHORT else 2

        def early_part(d):
            bank = psum.tile([P, R], F32, name="early", tag="out_bank")
            stage2(bank, d, range(early_groups(d)), 0, early_groups(d) - 1)
            nc.scalar.copy(out=result[d][:], in_=bank[:])

        def store(d):
            nc.sync.dma_start(out=out[P * d : P * (d + 1), :], in_=result[d][:])

        widen(0)
        widen(1)
        first_early, last_step = 8, TILES + 1
        done = OPEN
        for n in range(TILES + 2):
            if n % 2 == 0 and n < TILES:
                for s in (n, n + 1):
                    turn(s)
                    if s + 2 < TILES:
                        widen(s + 2)
            if n == 0:
                spread_lam()
            if n < TILES:
                product(n)
            if n == 0:
                interleave_b_hot()
            if 1 <= n <= TILES:
                quantise_dy(n - 1)
            if n == 2:
                quantise_b_hot()
            if n >= 2:
                stage1(n - 2)
            if n % PHASES == 1 and 5 <= n < TILES:
                weigh(n // PHASES - 1, nc.gpsimd, GPSIMD_WIDTH)
            if n % PHASES == 0 and 8 <= n <= TILES:
                quantise_g(n // PHASES - 2, R)
            while done - OPEN < (n + 1 - first_early) * (OUT_TILES - OPEN) // (last_step + 1 - first_early):
                early_part(done)
                done += 1

        weigh(GROUPS - 1, nc.vector, P)
        quantise_g(GROUPS - 1, P)

        waiting = []
        for d in range(OPEN):
            bank = psum.tile([P, R], F32, name="waiting_bank", tag="turned", bufs=4)
            stage2(bank, d, range(GROUPS - 1), 0, GROUPS - 1)
            waiting.append(bank)
        for i in range(OUT_TILES - OPEN):
            if i < OPEN:
                stage2(waiting[i], i, (GROUPS - 1,), 0, GROUPS - 1)
                nc.scalar.copy(out=result[i][:], in_=waiting[i][:])
                store(i)
            d = OPEN + i
            bank = psum.tile([P, R], F32, name="late", tag=("acc", "out_bank")[i % 2])
            stage2(bank, d, range(early_groups(d), GROUPS), early_groups(d), GROUPS - 1)
            nc.vector.tensor_tensor(out=result[d][:], in0=bank[:], in1=result[d][:], op=ADD)
            store(d)
